import numpy as np
import ml_dtypes


def mxq(x, axis, fmt="e4m3"):
    dtype, down = {"e4m3": (ml_dtypes.float8_e4m3fn, 7), "e5m2": (ml_dtypes.float8_e5m2, 14)}[fmt]
    v = np.moveaxis(np.asarray(x, np.float32).astype(ml_dtypes.bfloat16).astype(np.float64), axis, -1)
    blocks = v.reshape(v.shape[:-1] + (-1, 32))
    amax = np.abs(blocks).max(-1, keepdims=True)
    byte = np.maximum(np.where(amax > 0, np.frexp(amax)[1] - 1 + 127, 0) - down, 1)
    scale = np.exp2(byte - 127.0)
    codes = (blocks / scale).astype(np.float32).astype(dtype).astype(np.float64)
    return np.moveaxis((codes * scale).reshape(v.shape), -1, axis)


WIDE = False


def mx_kscale(k):
    if not WIDE:
        return np.ones(k)
    levels = np.array([10, -10, 5, -5, 0])
    if k % 512:
        return np.exp2(np.random.permutation(np.resize(levels, k // 32))).repeat(32)
    a = np.empty((k // 512, 16))
    for p in range(k // 512):
        a[p, :8] = np.random.permutation(np.resize(levels, 8))
        for g in range(8):
            far = levels[np.abs(levels - a[p, g]) >= 10]
            a[p, g + 8] = far[np.random.randint(len(far))]
    return np.exp2(a.ravel()).repeat(32)


def f64(x):
    return np.asarray(x).astype(np.float64)


def striped(idx):
    return np.tile(idx.reshape(-1, 16).T, (8, 1)).astype(np.uint16)


def unstriped(offs):
    return offs[:16].T.reshape(-1).astype(np.int64)


def pack_weight(w):
    k, n = w.shape
    w = f64(np.asarray(w, np.float32).astype(ml_dtypes.bfloat16)).reshape(k // 32, 32, n)
    amax = np.abs(w).max(1)
    byte = np.clip(np.where(amax > 0, np.frexp(amax)[1] - 1 + 127 - 7, 1), 1, 254)
    scaled = (w * np.exp2(127.0 - byte)[:, None, :]).reshape(k, n).astype(np.float32)
    words = np.ascontiguousarray(scaled.reshape(k // 512, 128, 4, n).transpose(0, 1, 3, 2)).astype(ml_dtypes.float8_e4m3fn).view(np.uint8)
    return words, np.ascontiguousarray(byte.astype(np.uint8).reshape(k // 512, 16, n))


def unpack_weight(words, scales):
    g, p, n, _ = words.shape
    vals = np.ascontiguousarray(words).view(ml_dtypes.float8_e4m3fn).astype(np.float64) * np.repeat(np.exp2(scales.astype(np.float64) - 127.0), 8, axis=1)[..., None]
    return vals.transpose(0, 1, 3, 2).reshape(g * 512, n)


def silu(v):
    return v / (1.0 + np.exp(-np.maximum(v, -700.0)))


K, T, S, V, H, N, J, U = 1024, 2048, 1024, 512, 512, 128, 512, 1024


def setup_inputs():
    n = np.random.standard_normal
    s = mx_kscale(K)[:, None]
    u = mx_kscale(H)
    r = mx_kscale(J)[:, None]
    packed_xT = pack_weight(n((K, T)) * s)
    return {
        "x_words": packed_xT[0],
        "x_scales": packed_xT[1],
        "aT": (n((J, U)) * r).astype(np.float32),
        "w1": (n((K, H)) / np.sqrt(K) / s * u).astype(np.float32),
        "w3": (n((J, H)) / np.sqrt(J) / r).astype(np.float32),
        "w2": (n((H, N)) / np.sqrt(2 * H) / u[:, None]).astype(np.float32),
        "offs": striped(np.random.permutation(T)[:S]),
        "pos1": striped(np.random.permutation(S)[:V]),
        "pos2": striped(np.random.permutation(S)[:V]),
    }


def reference(x_words, x_scales, aT, w1, w3, w2, offs, pos1, pos2):
    xq = unpack_weight(x_words, x_scales)[:, unstriped(offs)]
    h = silu(mxq(f64(w1), 0, "e4m3").T @ xq)
    f = mxq(f64(w3), 0, "e4m3").T @ mxq(f64(aT), 0, "e4m3")
    z = h[:, unstriped(pos1)] * f[:, :V] + h[:, unstriped(pos2)] * f[:, V:2 * V]
    return silu(mxq(f64(w2), 0, "e4m3").T @ mxq(z, 0, "e4m3"))

@@ -1,0 +1,209 @@
+from contextlib import ExitStack
+
+import concourse.mybir as mybir
+
+K, T, S, V, H, N, J, U = 1024, 2048, 1024, 512, 512, 128, 512, 1024
+FLOPS = 2 * (K * H * S + J * H * U + H * N * V)
+
+F32 = mybir.dt.float32
+BF16 = mybir.dt.bfloat16
+I32 = mybir.dt.int32
+U32 = mybir.dt.uint32
+U16 = mybir.dt.uint16
+U8 = mybir.dt.uint8
+FP8X4 = mybir.dt.float8_e4m3fn_x4
+MULT = mybir.AluOpType.mult
+ADD = mybir.AluOpType.add
+SILU = mybir.ActivationFunctionType.Silu
+
+P = 128
+PACK = 4
+BANK = 512
+CHUNK = 256
+
+
+def tile_picked_dime_silu_p_kernel(
+    tc, x_words, x_scales, aT, w1, w3, w2, offs, pos1, pos2, out
+):
+    nc = tc.nc
+    with ExitStack() as ctx:
+        sb = ctx.enter_context(tc.tile_pool(name="sb", bufs=1))
+        psum = ctx.enter_context(tc.psum_pool(name="psum", bufs=8))
+
+        def new(name, shape, dtype):
+            return sb.tile(shape, dtype, name=name, align_bytes=64)
+
+        def bank(name, shape):
+            return psum.tile(shape, F32, name=name, tag="bank")
+
+        def copy(engine, dst, src):
+            if engine == "S":
+                nc.scalar.copy(dst, src)
+            else:
+                nc.vector.tensor_copy(dst, src)
+
+        def quantize(name, grouped):
+            width = grouped.shape[1] // PACK
+            codes = new(name + "_codes", [P, width], U32)
+            scales = new(name + "_scales", [P, width], U8)
+            nc.vector.quantize_mx(out=codes[:].bitcast(FP8X4), scales=scales[:], in_=grouped[:])
+            return codes, scales
+
+        def mx(acc, stat, mov_codes, mov_scales, start, stop):
+            nc.tensor.matmul_mx(
+                out=acc, lhsT=stat[0][:].bitcast(FP8X4), lhsT_scale=stat[1][:],
+                rhs=mov_codes.bitcast(FP8X4), rhs_scale=mov_scales, start=start, stop=stop)
+
+        offs_sb = new("offs_sb", [P, S // 16], U16)
+        nc.sync.dma_start(offs_sb[:], offs)
+
+        xs_win = new("xs_win", [P, T], U8)
+        nc.vector.memset(xs_win[:].bitcast(I32), 0)
+        xs_i32 = x_scales.bitcast(I32)
+        for q in range(4):
+            nc.scalar.dma_start(xs_win[32 * q : 32 * q + 8, :].bitcast(I32), xs_i32[:, 4 * q : 4 * q + 4, :])
+        warm = new("warm", [P, 2], F32)
+        nc.vector.memset(warm[:, 0:1], 0.0)
+        nc.scalar.activation(warm[:, 1:2], warm[:, 0:1], SILU)
+
+        xw_win, w1_raw = [], []
+        for z in range(2):
+            win = new("xw_win%d" % z, [P, T], I32)
+            nc.sync.dma_start(win[:], x_words[z].rearrange("p c r -> p (c r)").bitcast(I32))
+            xw_win.append(win)
+            raw = new("w1_raw%d" % z, [P, PACK, H], F32)
+            nc.sync.dma_start(raw[:], w1[512 * z : 512 * (z + 1), :].rearrange("(p j) c -> p j c", j=PACK))
+            w1_raw.append(raw)
+        w3_raw = new("w3_raw", [P, PACK, H], F32)
+        nc.sync.dma_start(w3_raw[:], w3.rearrange("(p j) c -> p j c", j=PACK))
+        a_rows = aT.rearrange("(p j) c -> p j c", j=PACK)
+        a_raw, pos_sb = {}, []
+        for c in range(V // CHUNK):
+            for d in range(2):
+                raw = new("a_raw%d%d" % (c, d), [P, PACK, CHUNK], F32)
+                lo = V * d + CHUNK * c
+                nc.sync.dma_start(raw[:], a_rows[:, :, lo : lo + CHUNK])
+                a_raw[c, d] = raw
+                if c == 0:
+                    lst = new("pos_sb%d" % d, [P, V // 16], U16)
+                    nc.sync.dma_start(lst[:], (pos1, pos2)[d])
+                    pos_sb.append(lst)
+        w2_raw = new("w2_raw", [P, PACK, N], F32)
+        w2_rows = w2.rearrange("(g t i) n -> t g i n", t=PACK, i=4)
+        for t in range(PACK):
+            nc.sync.dma_start(w2_raw[:, t, :], w2_rows[t])
+
+        def cast_weights(name, raw, t, engine):
+            grouped = new(name, [P, P * PACK], BF16)
+            copy(engine,
+                 grouped[:].rearrange("p (g i j) -> p g j i", i=4, j=PACK),
+                 raw[:].rearrange("p j (g t i) -> p t g j i", t=PACK, i=4)[:, t])
+            return grouped
+
+        def cast_plain(name, raw, engine):
+            width = raw.shape[2]
+            grouped = new(name, [P, width * PACK], BF16)
+            copy(engine,
+                 grouped[:].rearrange("p (g i j) -> p g j i", i=4, j=PACK),
+                 raw[:].rearrange("p j (g i) -> p g j i", i=4))
+            return grouped
+
+        def gather_x(name, window, dtype, half):
+            picked = new(name, [P, BANK], dtype)
+            nc.vector.tensor_copy(picked[:], window.indirect(offs_sb[:, 32 * half : 32 * (half + 1)]))
+            return picked
+
+        xw, xs = {}, {}
+        for half in range(2):
+            xw[0, half] = gather_x("xw0%d" % half, xw_win[0][:].bitcast(U32), U32, half)
+        for half in range(2):
+            xs[half] = gather_x("xs%d" % half, xs_win[:], U8, half)
+        w1_bf = [cast_weights("w1bf0%d" % t, w1_raw[0], t, "S") for t in range(PACK)]
+        w1q = {}
+        for t in range(PACK):
+            w1q[0, t] = quantize("w1q0%d" % t, w1_bf[t])
+        h_acc = {}
+        for half in range(2):
+            for t in range(PACK):
+                h_acc[t, half] = None
+        for t in range(PACK):
+            for half in range(2):
+                h_acc[t, half] = bank("h_acc%d%d" % (t, half), [P, BANK])
+        for half in range(2):
+            for t in range(PACK):
+                mx(h_acc[t, half][:], w1q[0, t], xw[0, half][:], xs[half][:], True, False)
+        for half in range(2):
+            xw[1, half] = gather_x("xw1%d" % half, xw_win[1][:].bitcast(U32), U32, half)
+        w1_bf = [cast_weights("w1bf1%d" % t, w1_raw[1], t, "SSVV"[t]) for t in range(PACK)]
+        for t in range(PACK):
+            w1q[1, t] = quantize("w1q1%d" % t, w1_bf[t])
+        for t in range(PACK):
+            for half in range(2):
+                mx(h_acc[t, half][:], w1q[1, t], xw[1, half][:], xs[half][4:P, :], False, True)
+        h = [new("h%d" % t, [P, S], F32) for t in range(PACK)]
+
+        def silu_h(t):
+            for half in range(2):
+                nc.scalar.activation(h[t][:, BANK * half : BANK * (half + 1)], h_acc[t, half][:], SILU)
+
+        silu_h(0)
+        silu_h(1)
+
+        w3_bf = [cast_weights("w3bf%d" % t, w3_raw, t, "V") for t in range(PACK)]
+        w3q = [quantize("w3q%d" % t, w3_bf[t]) for t in range(PACK)]
+
+        def filters(c, d, engine, between):
+            a_codes, a_scales = quantize("aq%d%d" % (c, d), cast_plain("abf%d%d" % (c, d), a_raw[c, d], engine))
+            res = []
+            for pair in range(2):
+                acc = bank("f_acc%d%d%d" % (c, d, pair), [P, 2, CHUNK])
+                for e in range(2):
+                    mx(acc[:, e, :], w3q[2 * pair + e], a_codes[:], a_scales[:], True, True)
+                f_sb = new("f%d%d%d" % (c, d, pair), [P, 2, CHUNK], F32)
+                nc.scalar.copy(f_sb[:], acc[:])
+                res.extend([f_sb[:, 0, :], f_sb[:, 1, :]])
+                if between:
+                    silu_h(2 + pair)
+            return res
+
+        def messages(d, f, c, lo, width):
+            prod = new("m%d_%d" % (d, lo), [P, PACK, width], F32)
+            for t in range(PACK):
+                nc.vector.tensor_tensor(
+                    prod[:, t, :],
+                    h[t][:].indirect(pos_sb[d][:, lo // 16 : (lo + width) // 16]),
+                    f[t][:, lo - CHUNK * c : lo - CHUNK * c + width], MULT)
+            return prod
+
+        def add(lo, width, m0, m1):
+            z_bf = new("z_bf%d" % lo, [P, width * PACK], BF16)
+            nc.vector.tensor_tensor(
+                z_bf[:].rearrange("p (g i t) -> p g t i", i=2, t=PACK),
+                m0.rearrange("p t (g i) -> p g t i", i=2),
+                m1.rearrange("p t (g i) -> p g t i", i=2), ADD)
+            return z_bf
+
+        def project(lo, width, z_bf):
+            z_codes, z_scales = quantize("zq%d" % lo, z_bf)
+            acc = bank("o_acc%d" % lo, [P, width])
+            mx(acc[:], w2q, z_codes[:], z_scales[:], True, True)
+            res = new("res%d" % lo, [P, width], F32)
+            nc.scalar.activation(res[:], acc[:], SILU)
+            nc.sync.dma_start(out[:, lo : lo + width], res[:])
+
+        f00 = filters(0, 0, "V", True)
+        f01 = filters(0, 1, "S", False)
+        m00 = messages(0, f00, 0, 0, 256)
+        f10 = filters(1, 0, "S", False)
+        m01 = messages(1, f01, 0, 0, 256)
+        f11 = filters(1, 1, "S", False)
+        w2q = quantize("w2q", cast_plain("w2bf", w2_raw, "S"))
+        z0 = add(0, 256, m00[:], m01[:])
+        m10 = messages(0, f10, 1, 256, 256)
+        project(0, 256, z0)
+        m11a = messages(1, f11, 1, 256, 128)
+        z1 = add(256, 128, m10[:, :, 0:128], m11a[:])
+        m11b = messages(1, f11, 1, 384, 128)
+        project(256, 128, z1)
+        z2 = add(384, 128, m10[:, :, 128:256], m11b[:])
+        project(384, 128, z2)

@@ -1,6 +1,7 @@
 from contextlib import ExitStack
 
 import concourse.mybir as mybir
+from concourse.masks import make_identity
 
 K, T, S, V, H, N, J, U = 1024, 2048, 1024, 512, 512, 128, 512, 1024
 FLOPS = 2 * (K * H * S + J * H * U + H * N * V)
@@ -18,8 +19,14 @@ SILU = mybir.ActivationFunctionType.Silu
 
 P = 128
 PACK = 4
+K_PASS = P * PACK
 BANK = 512
-CHUNK = 256
+BANKS = 8
+RUN = 4
+LIST_ROWS = 16
+SCALE_ROWS = 4
+CHUNK = V // 2
+TAIL = CHUNK // 2
 
 
 def tile_picked_dime_silu_p_kernel(
@@ -27,20 +34,17 @@ def tile_picked_dime_silu_p_kernel(
 ):
     nc = tc.nc
     with ExitStack() as ctx:
-        sb = ctx.enter_context(tc.tile_pool(name="sb", bufs=1))
-        psum = ctx.enter_context(tc.psum_pool(name="psum", bufs=8))
+        sbuf = ctx.enter_context(tc.tile_pool(name="sbuf", bufs=1))
+        psum = ctx.enter_context(tc.psum_pool(name="psum", bufs=BANKS))
 
-        def new(name, shape, dtype):
-            return sb.tile(shape, dtype, name=name, align_bytes=64)
+        def new(name, shape, dtype, after=None):
+            return sbuf.tile(shape, dtype, name=name, tag=after or name, align_bytes=64)
 
         def bank(name, shape):
             return psum.tile(shape, F32, name=name, tag="bank")
 
-        def copy(engine, dst, src):
-            if engine == "S":
-                nc.scalar.copy(dst, src)
-            else:
-                nc.vector.tensor_copy(dst, src)
+        def entries(list_tile, lo, width):
+            return list_tile[:, lo // LIST_ROWS : (lo + width) // LIST_ROWS]
 
         def quantize(name, grouped):
             width = grouped.shape[1] // PACK
@@ -49,161 +53,193 @@ def tile_picked_dime_silu_p_kernel(
             nc.vector.quantize_mx(out=codes[:].bitcast(FP8X4), scales=scales[:], in_=grouped[:])
             return codes, scales
 
-        def mx(acc, stat, mov_codes, mov_scales, start, stop):
+        def stationaries(quantized):
+            codes, scales = quantized
+            return [(codes[:, lo : lo + P], scales[:, lo : lo + P]) for lo in range(0, codes.shape[1], P)]
+
+        def mx(acc, stationary, codes, scales, start, stop):
             nc.tensor.matmul_mx(
-                out=acc, lhsT=stat[0][:].bitcast(FP8X4), lhsT_scale=stat[1][:],
-                rhs=mov_codes.bitcast(FP8X4), rhs_scale=mov_scales, start=start, stop=stop)
+                out=acc, lhsT=stationary[0].bitcast(FP8X4), lhsT_scale=stationary[1],
+                rhs=codes.bitcast(FP8X4), rhs_scale=scales, start=start, stop=stop)
 
-        offs_sb = new("offs_sb", [P, S // 16], U16)
+        offs_sb = new("offs_sb", [P, S // LIST_ROWS], U16)
         nc.sync.dma_start(offs_sb[:], offs)
+        pos_sb = []
+        for d, pos in enumerate((pos1, pos2)):
+            pos_tile = new("pos_sb%d" % d, [P, V // LIST_ROWS], U16)
+            nc.sync.dma_start(pos_tile[:], pos)
+            pos_sb.append(pos_tile)
 
-        xs_win = new("xs_win", [P, T], U8)
-        nc.vector.memset(xs_win[:].bitcast(I32), 0)
-        xs_i32 = x_scales.bitcast(I32)
-        for q in range(4):
-            nc.scalar.dma_start(xs_win[32 * q : 32 * q + 8, :].bitcast(I32), xs_i32[:, 4 * q : 4 * q + 4, :])
-        warm = new("warm", [P, 2], F32)
-        nc.vector.memset(warm[:, 0:1], 0.0)
-        nc.scalar.activation(warm[:, 1:2], warm[:, 0:1], SILU)
+        scale_window = new("scale_window", [P, T], U8)
+        nc.vector.memset(scale_window[:].bitcast(I32), 0)
+        scale_rows = x_scales.bitcast(I32)
 
-        xw_win, w1_raw = [], []
-        for z in range(2):
-            win = new("xw_win%d" % z, [P, T], I32)
-            nc.sync.dma_start(win[:], x_words[z].rearrange("p c r -> p (c r)").bitcast(I32))
-            xw_win.append(win)
-            raw = new("w1_raw%d" % z, [P, PACK, H], F32)
-            nc.sync.dma_start(raw[:], w1[512 * z : 512 * (z + 1), :].rearrange("(p j) c -> p j c", j=PACK))
-            w1_raw.append(raw)
-        w3_raw = new("w3_raw", [P, PACK, H], F32)
-        nc.sync.dma_start(w3_raw[:], w3.rearrange("(p j) c -> p j c", j=PACK))
-        a_rows = aT.rearrange("(p j) c -> p j c", j=PACK)
-        a_raw, pos_sb = {}, []
-        for c in range(V // CHUNK):
-            for d in range(2):
-                raw = new("a_raw%d%d" % (c, d), [P, PACK, CHUNK], F32)
-                lo = V * d + CHUNK * c
-                nc.sync.dma_start(raw[:], a_rows[:, :, lo : lo + CHUNK])
-                a_raw[c, d] = raw
-                if c == 0:
-                    lst = new("pos_sb%d" % d, [P, V // 16], U16)
-                    nc.sync.dma_start(lst[:], (pos1, pos2)[d])
-                    pos_sb.append(lst)
-        w2_raw = new("w2_raw", [P, PACK, N], F32)
-        w2_rows = w2.rearrange("(g t i) n -> t g i n", t=PACK, i=4)
+        zero_in = new("zero_in", [P, 1], F32)
+        zero_add = new("zero_add", [P, 1], F32)
+        zero_bias = new("zero_bias", [P, 1], F32)
+        nc.gpsimd.memset(zero_in[:], 0.0)
+        nc.gpsimd.memset(zero_add[:], 0.0)
+        nc.scalar.activation(zero_bias[:], zero_in[:], SILU, bias=zero_add[:])
+        ident = new("ident", [P, P], F32)
+        make_identity(nc, ident[:])
+
+        def load_words(z, after=None):
+            window = new("word_window%d" % z, [P, T], I32, after)
+            nc.sync.dma_start(window[:], x_words[z].rearrange("p c r -> p (c r)").bitcast(I32))
+            return window
+
+        def load_rows(dst, rows):
+            view = dst.rearrange("p (j c) -> p j c", j=PACK)
+            nc.sync.dma_start(view, rows.rearrange("(p j) c -> p j c", j=PACK))
+            return view
+
+        word_windows = [load_words(0)]
+        for q in range(P // 32):
+            nc.sync.dma_start(scale_window[32 * q : 32 * q + 2 * SCALE_ROWS, :].bitcast(I32),
+                              scale_rows[:, SCALE_ROWS * q : SCALE_ROWS * (q + 1), :])
+
+        floats = new("floats", [P, PACK * (3 * H + U + N)], F32, "zero_add")
+        w3_at, a_at, w2_at, w1_first_at = PACK * H, PACK * 2 * H, PACK * (2 * H + U), PACK * (2 * H + U + N)
+        w1_raw = [load_rows(floats[:, w1_first_at:], w1[0:K_PASS, :])]
+        word_windows.append(load_words(1, "zero_in"))
+        w1_raw.append(load_rows(floats[:, 0:w3_at], w1[K_PASS:K, :]))
+        w3_raw = load_rows(floats[:, w3_at:a_at], w3)
+        a_raw = {}
+        for c, d in ((0, 1), (0, 0), (1, 0), (1, 1)):
+            lo = V * d + CHUNK * c
+            at = a_at + PACK * CHUNK * (2 * c + d)
+            a_raw[c, d] = load_rows(floats[:, at : at + PACK * CHUNK], aT[:, lo : lo + CHUNK])
+        w2_raw = floats[:, w2_at:w1_first_at].rearrange("p (t n) -> p t n", t=PACK)
+        w2_rows = w2.rearrange("(g t i) n -> t g i n", t=PACK, i=RUN)
         for t in range(PACK):
             nc.sync.dma_start(w2_raw[:, t, :], w2_rows[t])
 
-        def cast_weights(name, raw, t, engine):
-            grouped = new(name, [P, P * PACK], BF16)
-            copy(engine,
-                 grouped[:].rearrange("p (g i j) -> p g j i", i=4, j=PACK),
-                 raw[:].rearrange("p j (g t i) -> p t g j i", t=PACK, i=4)[:, t])
+        def cast_weights(name, raw, t0, count, copy):
+            grouped = new(name, [P, count * P * PACK], BF16)
+            copy(grouped[:].rearrange("p (t g i j) -> p t g j i", t=count, i=RUN, j=PACK),
+                 raw.rearrange("p j (g t i) -> p t g j i", t=PACK, i=RUN)[:, t0 : t0 + count])
             return grouped
 
-        def cast_plain(name, raw, engine):
-            width = raw.shape[2]
-            grouped = new(name, [P, width * PACK], BF16)
-            copy(engine,
-                 grouped[:].rearrange("p (g i j) -> p g j i", i=4, j=PACK),
-                 raw[:].rearrange("p j (g i) -> p g j i", i=4))
+        def cast_plain(name, raw, copy):
+            grouped = new(name, [P, raw.shape[2] * PACK], BF16)
+            copy(grouped[:].rearrange("p (g i j) -> p g j i", i=RUN, j=PACK),
+                 raw.rearrange("p j (g i) -> p g j i", i=RUN))
             return grouped
 
-        def gather_x(name, window, dtype, half):
-            picked = new(name, [P, BANK], dtype)
-            nc.vector.tensor_copy(picked[:], window.indirect(offs_sb[:, 32 * half : 32 * (half + 1)]))
+        def gather_x(name, window, dtype, after=None):
+            picked = new(name, [P, S], dtype, after)
+            nc.vector.tensor_copy(picked[:], window.indirect(offs_sb[:]))
             return picked
 
-        xw, xs = {}, {}
-        for half in range(2):
-            xw[0, half] = gather_x("xw0%d" % half, xw_win[0][:].bitcast(U32), U32, half)
-        for half in range(2):
-            xs[half] = gather_x("xs%d" % half, xs_win[:], U8, half)
-        w1_bf = [cast_weights("w1bf0%d" % t, w1_raw[0], t, "S") for t in range(PACK)]
-        w1q = {}
-        for t in range(PACK):
-            w1q[0, t] = quantize("w1q0%d" % t, w1_bf[t])
+        words0 = gather_x("words0", word_windows[0][:].bitcast(U32), U32)
+        x_scale = gather_x("x_scale", scale_window[:], U8)
         h_acc = {}
-        for half in range(2):
-            for t in range(PACK):
-                h_acc[t, half] = None
         for t in range(PACK):
             for half in range(2):
                 h_acc[t, half] = bank("h_acc%d%d" % (t, half), [P, BANK])
-        for half in range(2):
+
+        def layer_pass(z, words, second_copy):
+            w1q = stationaries(quantize("w1q%da" % z, cast_weights("w1bf%da" % z, w1_raw[z], 0, 2, nc.scalar.copy)))
+            w1q = w1q + stationaries(quantize("w1q%db" % z, cast_weights("w1bf%db" % z, w1_raw[z], 2, 2, second_copy)))
             for t in range(PACK):
-                mx(h_acc[t, half][:], w1q[0, t], xw[0, half][:], xs[half][:], True, False)
-        for half in range(2):
-            xw[1, half] = gather_x("xw1%d" % half, xw_win[1][:].bitcast(U32), U32, half)
-        w1_bf = [cast_weights("w1bf1%d" % t, w1_raw[1], t, "SSVV"[t]) for t in range(PACK)]
-        for t in range(PACK):
-            w1q[1, t] = quantize("w1q1%d" % t, w1_bf[t])
-        for t in range(PACK):
-            for half in range(2):
-                mx(h_acc[t, half][:], w1q[1, t], xw[1, half][:], xs[half][4:P, :], False, True)
+                for half in range(2):
+                    cols = slice(BANK * half, BANK * (half + 1))
+                    mx(h_acc[t, half][:], w1q[t], words[:, cols], x_scale[SCALE_ROWS * z : P, cols], z == 0, z == 1)
+
+        layer_pass(0, words0, nc.scalar.copy)
+        layer_pass(1, gather_x("words1", word_windows[1][:].bitcast(U32), U32, "scale_window"), nc.vector.tensor_copy)
         h = [new("h%d" % t, [P, S], F32) for t in range(PACK)]
-
-        def silu_h(t):
+        for t in range(PACK):
             for half in range(2):
-                nc.scalar.activation(h[t][:, BANK * half : BANK * (half + 1)], h_acc[t, half][:], SILU)
+                nc.scalar.activation(h[t][:, BANK * half : BANK * (half + 1)], h_acc[t, half][:], SILU, bias=zero_bias[:])
 
-        silu_h(0)
-        silu_h(1)
+        w3q = stationaries(quantize("w3q", cast_weights("w3bf", w3_raw, 0, PACK, nc.vector.tensor_copy)))
 
-        w3_bf = [cast_weights("w3bf%d" % t, w3_raw, t, "V") for t in range(PACK)]
-        w3q = [quantize("w3q%d" % t, w3_bf[t]) for t in range(PACK)]
-
-        def filters(c, d, engine, between):
-            a_codes, a_scales = quantize("aq%d%d" % (c, d), cast_plain("abf%d%d" % (c, d), a_raw[c, d], engine))
-            res = []
+        def filter_banks(c, d, copy):
+            a_codes, a_scales = quantize("aq%d%d" % (c, d), cast_plain("abf%d%d" % (c, d), a_raw[c, d], copy))
+            banks = []
             for pair in range(2):
                 acc = bank("f_acc%d%d%d" % (c, d, pair), [P, 2, CHUNK])
                 for e in range(2):
                     mx(acc[:, e, :], w3q[2 * pair + e], a_codes[:], a_scales[:], True, True)
-                f_sb = new("f%d%d%d" % (c, d, pair), [P, 2, CHUNK], F32)
-                nc.scalar.copy(f_sb[:], acc[:])
-                res.extend([f_sb[:, 0, :], f_sb[:, 1, :]])
-                if between:
-                    silu_h(2 + pair)
-            return res
+                banks.append(acc)
+            return banks
 
-        def messages(d, f, c, lo, width):
-            prod = new("m%d_%d" % (d, lo), [P, PACK, width], F32)
-            for t in range(PACK):
+        def to_sbuf(name, banks):
+            tiles = []
+            for pair, acc in enumerate(banks):
+                f_sb = new("%s_%d" % (name, pair), [P, 2, CHUNK], F32)
+                nc.scalar.copy(f_sb[:], acc[:])
+                tiles.extend([f_sb[:, 0, :], f_sb[:, 1, :]])
+            return tiles
+
+        def products(name, d, f, lo, width, t0, count, after=None):
+            prod = new(name, [P, count, width], F32, after)
+            for e in range(count):
                 nc.vector.tensor_tensor(
-                    prod[:, t, :],
-                    h[t][:].indirect(pos_sb[d][:, lo // 16 : (lo + width) // 16]),
-                    f[t][:, lo - CHUNK * c : lo - CHUNK * c + width], MULT)
+                    prod[:, e, :], h[t0 + e][:].indirect(entries(pos_sb[d], lo, width)),
+                    f[t0 + e][:, lo % CHUNK : lo % CHUNK + width], MULT)
             return prod
 
-        def add(lo, width, m0, m1):
-            z_bf = new("z_bf%d" % lo, [P, width * PACK], BF16)
+        def add_on_vector(name, m0, m1):
+            z_bf = new(name, [P, m0.shape[2] * PACK], BF16)
             nc.vector.tensor_tensor(
                 z_bf[:].rearrange("p (g i t) -> p g t i", i=2, t=PACK),
                 m0.rearrange("p t (g i) -> p g t i", i=2),
                 m1.rearrange("p t (g i) -> p g t i", i=2), ADD)
             return z_bf
 
-        def project(lo, width, z_bf):
+        def add_on_tensor(name, m0, m1):
+            z_bf = new(name, [P, CHUNK * PACK], BF16)
+            sums = [bank("zt_acc%d" % b, [P, PACK, P]) for b in range(CHUNK // P)]
+            for term, m in enumerate((m0, m1)):
+                for t in range(PACK):
+                    for b, acc in enumerate(sums):
+                        nc.tensor.matmul(acc[:, t, :], m[t][:, P * b : P * (b + 1)], ident[:], is_transpose=True,
+                                         start=(term == 0 and t == 0), stop=(term == 1 and t == PACK - 1))
+            for b, acc in enumerate(sums):
+                zt = new("zt%d" % b, [P, PACK * P], BF16)
+                nc.scalar.copy(zt[:].rearrange("v (u p e) -> v u p e", u=2, e=2),
+                               acc[:].rearrange("v (u e) p -> v u p e", e=2))
+                back = bank("back%d" % b, [P, 2, P])
+                for u in range(2):
+                    nc.tensor.transpose(back[:, u, :], zt[:].bitcast(F32)[:, P * u : P * (u + 1)], ident[:])
+                nc.scalar.copy(z_bf[:, PACK * P * b : PACK * P * (b + 1)].bitcast(F32).rearrange("p (v u) -> p v u", u=2),
+                               back[:].rearrange("p u v -> p v u"))
+            return z_bf
+
+        def project(lo, z_bf):
             z_codes, z_scales = quantize("zq%d" % lo, z_bf)
+            width = z_codes.shape[1]
             acc = bank("o_acc%d" % lo, [P, width])
             mx(acc[:], w2q, z_codes[:], z_scales[:], True, True)
-            res = new("res%d" % lo, [P, width], F32)
-            nc.scalar.activation(res[:], acc[:], SILU)
-            nc.sync.dma_start(out[:, lo : lo + width], res[:])
+            result = new("result%d" % lo, [P, width], F32)
+            nc.scalar.activation(result[:], acc[:], SILU, bias=zero_bias[:])
+            nc.sync.dma_start(out[:, lo : lo + width], result[:])
 
-        f00 = filters(0, 0, "V", True)
-        f01 = filters(0, 1, "S", False)
-        m00 = messages(0, f00, 0, 0, 256)
-        f10 = filters(1, 0, "S", False)
-        m01 = messages(1, f01, 0, 0, 256)
-        f11 = filters(1, 1, "S", False)
-        w2q = quantize("w2q", cast_plain("w2bf", w2_raw, "S"))
-        z0 = add(0, 256, m00[:], m01[:])
-        m10 = messages(0, f10, 1, 256, 256)
-        project(0, 256, z0)
-        m11a = messages(1, f11, 1, 256, 128)
-        z1 = add(256, 128, m10[:, :, 0:128], m11a[:])
-        m11b = messages(1, f11, 1, 384, 128)
-        project(256, 128, z1)
-        z2 = add(384, 128, m10[:, :, 128:256], m11b[:])
-        project(384, 128, z2)
+        f01 = to_sbuf("f01", filter_banks(0, 1, nc.vector.tensor_copy))
+        h00 = new("h00", [P, PACK, CHUNK], F32, "abf01")
+        for t in range(PACK):
+            nc.vector.tensor_copy(h00[:, t, :], h[t][:].indirect(entries(pos_sb[0], 0, CHUNK)))
+        f00_banks = filter_banks(0, 0, nc.scalar.copy)
+        m01_low = products("m01_low", 1, f01, 0, CHUNK, 0, 2)
+        m01_high = products("m01_high", 1, f01, 0, CHUNK, 2, 2, "abf00")
+        f10_banks = filter_banks(1, 0, nc.scalar.copy)
+        m00 = new("m00", [P, PACK, CHUNK], F32, "abf10")
+        for pair in range(2):
+            both = slice(2 * pair, 2 * pair + 2)
+            nc.vector.tensor_tensor(m00[:, both, :], h00[:, both, :], f00_banks[pair][:], MULT)
+        f11_banks = filter_banks(1, 1, nc.scalar.copy)
+        f10 = to_sbuf("f10", f10_banks)
+        f11 = to_sbuf("f11", f11_banks)
+        w2q = stationaries(quantize("w2q", cast_plain("w2bf", w2_raw, nc.scalar.copy)))[0]
+        z_first = add_on_tensor("z_first", [m[:, e, :] for m in (m01_low, m01_high) for e in range(2)],
+                                [m00[:, t, :] for t in range(PACK)])
+        m10 = products("m10", 0, f10, CHUNK, CHUNK, 0, PACK, "abf11")
+        project(0, z_first)
+        m11_head = products("m11_head", 1, f11, CHUNK, TAIL, 0, PACK)
+        z_second = add_on_vector("z_second", m10[:, :, 0:TAIL], m11_head[:])
+        m11_tail = products("m11_tail", 1, f11, CHUNK + TAIL, TAIL, 0, PACK, "z_first")
+        project(CHUNK, z_second)
+        z_third = add_on_vector("z_third", m10[:, :, TAIL:CHUNK], m11_tail[:])
+        project(CHUNK + TAIL, z_third)

from contextlib import ExitStack

import concourse.mybir as mybir
from concourse.masks import make_identity

K, T, S, V, H, N, J, U = 1024, 2048, 1024, 512, 512, 128, 512, 1024
FLOPS = 2 * (K * H * S + J * H * U + H * N * V)

F32 = mybir.dt.float32
BF16 = mybir.dt.bfloat16
I32 = mybir.dt.int32
U32 = mybir.dt.uint32
U16 = mybir.dt.uint16
U8 = mybir.dt.uint8
FP8X4 = mybir.dt.float8_e4m3fn_x4
MULT = mybir.AluOpType.mult
ADD = mybir.AluOpType.add
SILU = mybir.ActivationFunctionType.Silu

P = 128
PACK = 4
K_PASS = P * PACK
BANK = 512
BANKS = 8
RUN = 4
LIST_ROWS = 16
SCALE_ROWS = 4
CHUNK = V // 2
TAIL = CHUNK // 2


def tile_picked_dime_silu_p_kernel(
    tc, x_words, x_scales, aT, w1, w3, w2, offs, pos1, pos2, out
):
    nc = tc.nc
    with ExitStack() as ctx:
        sbuf = ctx.enter_context(tc.tile_pool(name="sbuf", bufs=1))
        psum = ctx.enter_context(tc.psum_pool(name="psum", bufs=BANKS))

        def new(name, shape, dtype, after=None):
            return sbuf.tile(shape, dtype, name=name, tag=after or name, align_bytes=64)

        def bank(name, shape):
            return psum.tile(shape, F32, name=name, tag="bank")

        def entries(list_tile, lo, width):
            return list_tile[:, lo // LIST_ROWS : (lo + width) // LIST_ROWS]

        def quantize(name, grouped):
            width = grouped.shape[1] // PACK
            codes = new(name + "_codes", [P, width], U32)
            scales = new(name + "_scales", [P, width], U8)
            nc.vector.quantize_mx(out=codes[:].bitcast(FP8X4), scales=scales[:], in_=grouped[:])
            return codes, scales

        def stationaries(quantized):
            codes, scales = quantized
            return [(codes[:, lo : lo + P], scales[:, lo : lo + P]) for lo in range(0, codes.shape[1], P)]

        def mx(acc, stationary, codes, scales, start, stop):
            nc.tensor.matmul_mx(
                out=acc, lhsT=stationary[0].bitcast(FP8X4), lhsT_scale=stationary[1],
                rhs=codes.bitcast(FP8X4), rhs_scale=scales, start=start, stop=stop)

        offs_sb = new("offs_sb", [P, S // LIST_ROWS], U16)
        nc.sync.dma_start(offs_sb[:], offs)
        pos_sb = []
        for d, pos in enumerate((pos1, pos2)):
            pos_tile = new("pos_sb%d" % d, [P, V // LIST_ROWS], U16)
            nc.sync.dma_start(pos_tile[:], pos)
            pos_sb.append(pos_tile)

        scale_window = new("scale_window", [P, T], U8)
        nc.vector.memset(scale_window[:].bitcast(I32), 0)
        scale_rows = x_scales.bitcast(I32)

        zero_in = new("zero_in", [P, 1], F32)
        zero_add = new("zero_add", [P, 1], F32)
        zero_bias = new("zero_bias", [P, 1], F32)
        nc.gpsimd.memset(zero_in[:], 0.0)
        nc.gpsimd.memset(zero_add[:], 0.0)
        nc.scalar.activation(zero_bias[:], zero_in[:], SILU, bias=zero_add[:])
        ident = new("ident", [P, P], F32)
        make_identity(nc, ident[:])

        def load_words(z, after=None):
            window = new("word_window%d" % z, [P, T], I32, after)
            nc.sync.dma_start(window[:], x_words[z].rearrange("p c r -> p (c r)").bitcast(I32))
            return window

        def load_rows(dst, rows):
            view = dst.rearrange("p (j c) -> p j c", j=PACK)
            nc.sync.dma_start(view, rows.rearrange("(p j) c -> p j c", j=PACK))
            return view

        word_windows = [load_words(0)]
        for q in range(P // 32):
            nc.sync.dma_start(scale_window[32 * q : 32 * q + 2 * SCALE_ROWS, :].bitcast(I32),
                              scale_rows[:, SCALE_ROWS * q : SCALE_ROWS * (q + 1), :])

        floats = new("floats", [P, PACK * (3 * H + U + N)], F32, "zero_add")
        w3_at, a_at, w2_at, w1_first_at = PACK * H, PACK * 2 * H, PACK * (2 * H + U), PACK * (2 * H + U + N)
        w1_raw = [load_rows(floats[:, w1_first_at:], w1[0:K_PASS, :])]
        word_windows.append(load_words(1, "zero_in"))
        w1_raw.append(load_rows(floats[:, 0:w3_at], w1[K_PASS:K, :]))
        w3_raw = load_rows(floats[:, w3_at:a_at], w3)
        a_raw = {}
        for c, d in ((0, 1), (0, 0), (1, 0), (1, 1)):
            lo = V * d + CHUNK * c
            at = a_at + PACK * CHUNK * (2 * c + d)
            a_raw[c, d] = load_rows(floats[:, at : at + PACK * CHUNK], aT[:, lo : lo + CHUNK])
        w2_raw = floats[:, w2_at:w1_first_at].rearrange("p (t n) -> p t n", t=PACK)
        w2_rows = w2.rearrange("(g t i) n -> t g i n", t=PACK, i=RUN)
        for t in range(PACK):
            nc.sync.dma_start(w2_raw[:, t, :], w2_rows[t])

        def cast_weights(name, raw, t0, count, copy):
            grouped = new(name, [P, count * P * PACK], BF16)
            copy(grouped[:].rearrange("p (t g i j) -> p t g j i", t=count, i=RUN, j=PACK),
                 raw.rearrange("p j (g t i) -> p t g j i", t=PACK, i=RUN)[:, t0 : t0 + count])
            return grouped

        def cast_plain(name, raw, copy):
            grouped = new(name, [P, raw.shape[2] * PACK], BF16)
            copy(grouped[:].rearrange("p (g i j) -> p g j i", i=RUN, j=PACK),
                 raw.rearrange("p j (g i) -> p g j i", i=RUN))
            return grouped

        def gather_x(name, window, dtype, after=None):
            picked = new(name, [P, S], dtype, after)
            nc.vector.tensor_copy(picked[:], window.indirect(offs_sb[:]))
            return picked

        words0 = gather_x("words0", word_windows[0][:].bitcast(U32), U32)
        x_scale = gather_x("x_scale", scale_window[:], U8)
        h_acc = {}
        for t in range(PACK):
            for half in range(2):
                h_acc[t, half] = bank("h_acc%d%d" % (t, half), [P, BANK])

        def layer_pass(z, words, second_copy):
            w1q = stationaries(quantize("w1q%da" % z, cast_weights("w1bf%da" % z, w1_raw[z], 0, 2, nc.scalar.copy)))
            w1q = w1q + stationaries(quantize("w1q%db" % z, cast_weights("w1bf%db" % z, w1_raw[z], 2, 2, second_copy)))
            for t in range(PACK):
                for half in range(2):
                    cols = slice(BANK * half, BANK * (half + 1))
                    mx(h_acc[t, half][:], w1q[t], words[:, cols], x_scale[SCALE_ROWS * z : P, cols], z == 0, z == 1)

        layer_pass(0, words0, nc.scalar.copy)
        layer_pass(1, gather_x("words1", word_windows[1][:].bitcast(U32), U32, "scale_window"), nc.vector.tensor_copy)
        h = [new("h%d" % t, [P, S], F32) for t in range(PACK)]
        for t in range(PACK):
            for half in range(2):
                nc.scalar.activation(h[t][:, BANK * half : BANK * (half + 1)], h_acc[t, half][:], SILU, bias=zero_bias[:])

        w3q = stationaries(quantize("w3q", cast_weights("w3bf", w3_raw, 0, PACK, nc.vector.tensor_copy)))

        def filter_banks(c, d, copy):
            a_codes, a_scales = quantize("aq%d%d" % (c, d), cast_plain("abf%d%d" % (c, d), a_raw[c, d], copy))
            banks = []
            for pair in range(2):
                acc = bank("f_acc%d%d%d" % (c, d, pair), [P, 2, CHUNK])
                for e in range(2):
                    mx(acc[:, e, :], w3q[2 * pair + e], a_codes[:], a_scales[:], True, True)
                banks.append(acc)
            return banks

        def to_sbuf(name, banks):
            tiles = []
            for pair, acc in enumerate(banks):
                f_sb = new("%s_%d" % (name, pair), [P, 2, CHUNK], F32)
                nc.scalar.copy(f_sb[:], acc[:])
                tiles.extend([f_sb[:, 0, :], f_sb[:, 1, :]])
            return tiles

        def products(name, d, f, lo, width, t0, count, after=None):
            prod = new(name, [P, count, width], F32, after)
            for e in range(count):
                nc.vector.tensor_tensor(
                    prod[:, e, :], h[t0 + e][:].indirect(entries(pos_sb[d], lo, width)),
                    f[t0 + e][:, lo % CHUNK : lo % CHUNK + width], MULT)
            return prod

        def add_on_vector(name, m0, m1):
            z_bf = new(name, [P, m0.shape[2] * PACK], BF16)
            nc.vector.tensor_tensor(
                z_bf[:].rearrange("p (g i t) -> p g t i", i=2, t=PACK),
                m0.rearrange("p t (g i) -> p g t i", i=2),
                m1.rearrange("p t (g i) -> p g t i", i=2), ADD)
            return z_bf

        def add_on_tensor(name, m0, m1):
            z_bf = new(name, [P, CHUNK * PACK], BF16)
            sums = [bank("zt_acc%d" % b, [P, PACK, P]) for b in range(CHUNK // P)]
            for term, m in enumerate((m0, m1)):
                for t in range(PACK):
                    for b, acc in enumerate(sums):
                        nc.tensor.matmul(acc[:, t, :], m[t][:, P * b : P * (b + 1)], ident[:], is_transpose=True,
                                         start=(term == 0 and t == 0), stop=(term == 1 and t == PACK - 1))
            for b, acc in enumerate(sums):
                zt = new("zt%d" % b, [P, PACK * P], BF16)
                nc.scalar.copy(zt[:].rearrange("v (u p e) -> v u p e", u=2, e=2),
                               acc[:].rearrange("v (u e) p -> v u p e", e=2))
                back = bank("back%d" % b, [P, 2, P])
                for u in range(2):
                    nc.tensor.transpose(back[:, u, :], zt[:].bitcast(F32)[:, P * u : P * (u + 1)], ident[:])
                nc.scalar.copy(z_bf[:, PACK * P * b : PACK * P * (b + 1)].bitcast(F32).rearrange("p (v u) -> p v u", u=2),
                               back[:].rearrange("p u v -> p v u"))
            return z_bf

        def project(lo, z_bf):
            z_codes, z_scales = quantize("zq%d" % lo, z_bf)
            width = z_codes.shape[1]
            acc = bank("o_acc%d" % lo, [P, width])
            mx(acc[:], w2q, z_codes[:], z_scales[:], True, True)
            result = new("result%d" % lo, [P, width], F32)
            nc.scalar.activation(result[:], acc[:], SILU, bias=zero_bias[:])
            nc.sync.dma_start(out[:, lo : lo + width], result[:])

        f01 = to_sbuf("f01", filter_banks(0, 1, nc.vector.tensor_copy))
        h00 = new("h00", [P, PACK, CHUNK], F32, "abf01")
        for t in range(PACK):
            nc.vector.tensor_copy(h00[:, t, :], h[t][:].indirect(entries(pos_sb[0], 0, CHUNK)))
        f00_banks = filter_banks(0, 0, nc.scalar.copy)
        m01_low = products("m01_low", 1, f01, 0, CHUNK, 0, 2)
        m01_high = products("m01_high", 1, f01, 0, CHUNK, 2, 2, "abf00")
        f10_banks = filter_banks(1, 0, nc.scalar.copy)
        m00 = new("m00", [P, PACK, CHUNK], F32, "abf10")
        for pair in range(2):
            both = slice(2 * pair, 2 * pair + 2)
            nc.vector.tensor_tensor(m00[:, both, :], h00[:, both, :], f00_banks[pair][:], MULT)
        f11_banks = filter_banks(1, 1, nc.scalar.copy)
        f10 = to_sbuf("f10", f10_banks)
        f11 = to_sbuf("f11", f11_banks)
        w2q = stationaries(quantize("w2q", cast_plain("w2bf", w2_raw, nc.scalar.copy)))[0]
        z_first = add_on_tensor("z_first", [m[:, e, :] for m in (m01_low, m01_high) for e in range(2)],
                                [m00[:, t, :] for t in range(PACK)])
        m10 = products("m10", 0, f10, CHUNK, CHUNK, 0, PACK, "abf11")
        project(0, z_first)
        m11_head = products("m11_head", 1, f11, CHUNK, TAIL, 0, PACK)
        z_second = add_on_vector("z_second", m10[:, :, 0:TAIL], m11_head[:])
        m11_tail = products("m11_tail", 1, f11, CHUNK + TAIL, TAIL, 0, PACK, "z_first")
        project(CHUNK, z_second)
        z_third = add_on_vector("z_third", m10[:, :, TAIL:CHUNK], m11_tail[:])
        project(CHUNK + TAIL, z_third)
